import numpy as np, ml_dtypes
CORES = [3,67,11,75,19,83,27,91,35,99,43,107,51,115,59,123]
N = 16
def setup_inputs(rng):
    return {"x": rng.standard_normal((N, 128, 256), dtype=np.float32).astype(ml_dtypes.bfloat16)}
def reference(x):
    s = np.cumsum(x.astype(np.float64), axis=0)
    return {"y": s.astype(x.dtype)}

from concourse.bass import DstId, RemoteDMATransfer

N = 16
SCRATCH = {
    "xs": ("dram", [N, 128, 16], "bfloat16"),
    "gather": ("dram", [N, 128, 16], "bfloat16"),
    "ys": ("dram", [N, 128, 16], "bfloat16"),
}
SEMAPHORES = ["loaded", "sent", "arrived", "back", "stored"]


def owner_core(T, o):
    return T.cores[o] + 4


def dst_id(topo, c):
    rid, pid, _sengine = topo.addr(c)
    return DstId(rid=rid, pnc=pid)


def rank_side(g, rank, T, topo):
    if rank == 0:
        g.scalar.dma_start(T.y[:], T.x[:]).then_inc(T.sem.stored, 16)
    g.sync.dma_start(T.xs[:], T.x[:]).then_inc(T.sem.loaded, 16)
    g.wait_ge(T.sem.loaded, 16)
    for first in (0, 8):
        g.remote_dma_fused(
            [RemoteDMATransfer(dst_ids=[dst_id(topo, owner_core(T, o))], dma_engine_mask=1 << (o - first),
                               remote_sem=T.sem.arrived, src=T.xs[o], dst=T.gather[rank])
             for o in range(first, first + 8)],
            local_sem=T.sem.sent)
    if rank > 0:
        g.sync.wait_ge(T.sem.back, N)
        g.sync.dma_start(T.y[:], T.ys[:]).then_inc(T.sem.stored, 16)
    g.wait_ge(T.sem.sent, N)
    g.wait_ge(T.sem.stored, 16)


def owner_side(g, o, T, topo):
    g.wait_ge(T.sem.arrived, N)
    calls = [[(15 - e, e) for e in range(8)], [(1 + e, e) for e in range(7)]]
    for call in calls:
        g.remote_dma_fused(
            [RemoteDMATransfer(dst_ids=[dst_id(topo, T.cores[r])], dma_engine_mask=1 << e,
                               remote_sem=T.sem.back, srcs=[T.gather[k] for k in range(r + 1)], dsts=[T.ys[o]],
                               alu_op=1)
             for r, e in call],
            local_sem=T.sem.sent)
    g.wait_ge(T.sem.sent, N - 1)


def rank_program(g, core, T, topo):
    owners = [owner_core(T, o) for o in range(N)]
    for a in range(N):
        for b in range(N):
            assert topo.may_write(T.cores[a], owners[b]) and topo.may_write(owners[b], T.cores[a])
            assert topo.die(T.cores[a]) != topo.die(owners[b])
    rank = T.rank_of(core)
    if rank is not None:
        rank_side(g, rank, T, topo)
    elif core in owners:
        owner_side(g, owners.index(core), T, topo)
